import numpy as np
import ml_dtypes


def mxq(x, axis, fmt="e4m3"):
    dtype, down = {"e4m3": (ml_dtypes.float8_e4m3fn, 7), "e5m2": (ml_dtypes.float8_e5m2, 14)}[fmt]
    v = np.moveaxis(np.asarray(x, np.float32).astype(ml_dtypes.bfloat16).astype(np.float64), axis, -1)
    blocks = v.reshape(v.shape[:-1] + (-1, 32))
    amax = np.abs(blocks).max(-1, keepdims=True)
    byte = np.maximum(np.where(amax > 0, np.frexp(amax)[1] - 1 + 127, 0) - down, 1)
    scale = np.exp2(byte - 127.0)
    codes = (blocks / scale).astype(np.float32).astype(dtype).astype(np.float64)
    return np.moveaxis((codes * scale).reshape(v.shape), -1, axis)


WIDE = False


def mx_kscale(k):
    if not WIDE:
        return np.ones(k)
    levels = np.array([10, -10, 5, -5, 0])
    if k % 512:
        return np.exp2(np.random.permutation(np.resize(levels, k // 32))).repeat(32)
    a = np.empty((k // 512, 16))
    for p in range(k // 512):
        a[p, :8] = np.random.permutation(np.resize(levels, 8))
        for g in range(8):
            far = levels[np.abs(levels - a[p, g]) >= 10]
            a[p, g + 8] = far[np.random.randint(len(far))]
    return np.exp2(a.ravel()).repeat(32)


def f64(x):
    return np.asarray(x).astype(np.float64)


def striped(idx):
    return np.tile(idx.reshape(-1, 16).T, (8, 1)).astype(np.uint16)


def unstriped(offs):
    return offs[:16].T.reshape(-1).astype(np.int64)


def pack_weight(w):
    k, n = w.shape
    w = f64(np.asarray(w, np.float32).astype(ml_dtypes.bfloat16)).reshape(k // 32, 32, n)
    amax = np.abs(w).max(1)
    byte = np.clip(np.where(amax > 0, np.frexp(amax)[1] - 1 + 127 - 7, 1), 1, 254)
    scaled = (w * np.exp2(127.0 - byte)[:, None, :]).reshape(k, n).astype(np.float32)
    words = np.ascontiguousarray(scaled.reshape(k // 512, 128, 4, n).transpose(0, 1, 3, 2)).astype(ml_dtypes.float8_e4m3fn).view(np.uint8)
    return words, np.ascontiguousarray(byte.astype(np.uint8).reshape(k // 512, 16, n))


def unpack_weight(words, scales):
    g, p, n, _ = words.shape
    vals = np.ascontiguousarray(words).view(ml_dtypes.float8_e4m3fn).astype(np.float64) * np.repeat(np.exp2(scales.astype(np.float64) - 127.0), 8, axis=1)[..., None]
    return vals.transpose(0, 1, 3, 2).reshape(g * 512, n)


def sigmoid(v):
    return 1.0 / (1.0 + np.exp(-np.maximum(v, -700.0)))


K, T, S, V, N = 1024, 2048, 768, 384, 128


def setup_inputs():
    n = np.random.standard_normal
    s = mx_kscale(K)[:, None]
    packed_xT = pack_weight(n((K, T)) * s)
    return {
        "x_words": packed_xT[0],
        "x_scales": packed_xT[1],
        "w1": (n((K, N)) / np.sqrt(K) / s).astype(np.float32),
        "offs": striped(np.random.permutation(T)[:S]),
    }


def reference(x_words, x_scales, w1, offs):
    xq = unpack_weight(x_words, x_scales)[:, unstriped(offs)]
    y = sigmoid(mxq(f64(w1), 0, "e4m3").T @ xq)
    return y[:, :V] * y[:, V:2 * V]

@@ -1,0 +1,112 @@
+from contextlib import ExitStack
+
+import concourse.mybir as mybir
+
+K, T, S, V, M = 1024, 2048, 768, 384, 128
+FLOPS = 2 * K * M * S
+
+F32 = mybir.dt.float32
+BF16 = mybir.dt.bfloat16
+I32 = mybir.dt.int32
+U32 = mybir.dt.uint32
+U16 = mybir.dt.uint16
+U8 = mybir.dt.uint8
+FP8X4 = mybir.dt.float8_e4m3fn_x4
+SIGMOID = mybir.ActivationFunctionType.Sigmoid
+
+P = 128
+PACK = 4
+PASSES = K // (P * PACK)
+QUADRANT = 32
+ROWS = 4
+STRIPE = 16
+GATHER = 256
+BLOCK = 128
+
+
+def tile_picked_andpool_none_p_kernel(tc, x_words, x_scales, w1, offs, out):
+    nc = tc.nc
+    with ExitStack() as ctx:
+        keep = ctx.enter_context(tc.tile_pool(name="keep", bufs=1))
+        psum = ctx.enter_context(tc.psum_pool(name="psum", bufs=1))
+
+        offsets = keep.tile([P, S // STRIPE], U16, name="offsets")
+        x_table = [keep.tile([P, T], I32, name="x_table%d" % z) for z in range(PASSES)]
+        scale_table = keep.tile([P, T], U8, name="scale_table")
+        w_raw = keep.tile([P, PASSES, PACK, M], F32, name="w_raw")
+
+        def load_words(z):
+            nc.sync.dma_start(out=x_table[z][:], in_=x_words[z].rearrange("p c t -> p (c t)").bitcast(I32))
+
+        def load_scales(q, queue):
+            queue.dma_start(
+                out=scale_table[QUADRANT * q : QUADRANT * q + PASSES * ROWS, :].bitcast(I32),
+                in_=x_scales[:, ROWS * q : ROWS * (q + 1), :].bitcast(I32),
+            )
+
+        def load_w():
+            nc.sync.dma_start(out=w_raw[:], in_=w1.rearrange("(z p t) m -> p z t m", p=P, t=PACK))
+
+        nc.vector.memset(scale_table[:].bitcast(I32), 0)
+        nc.sync.dma_start(offsets[:], offs)
+        load_words(0)
+        for q in range(P // QUADRANT):
+            load_scales(q, nc.sync)
+        load_w()
+        load_words(1)
+
+        warm_in = keep.tile([P, 1], F32, name="warm_in")
+        warm_out = keep.tile([P, 1], F32, name="warm_out")
+        nc.vector.memset(warm_in[:], 0.0)
+        nc.scalar.activation(out=warm_out[:], in_=warm_in[:], func=SIGMOID)
+
+        x_codes0 = keep.tile([P, S], U32, name="x_codes0", align_bytes=64)
+        nc.vector.tensor_copy(out=x_codes0[:], in_=x_table[0][:].bitcast(U32).indirect(offsets[:]))
+        x_planes = keep.tile([P, S], U8, name="x_planes", align_bytes=64)
+        nc.vector.tensor_copy(out=x_planes[:], in_=scale_table[:].indirect(offsets[:]))
+
+        w_grouped = keep.tile([P, PASSES, M, PACK], BF16, name="w_grouped", align_bytes=64)
+        nc.scalar.copy(out=w_grouped[:], in_=w_raw[:].rearrange("p z t m -> p z m t"))
+        w_codes = keep.tile([P, PASSES * M], U32, name="w_codes", align_bytes=64)
+        w_plane = keep.tile([P, PASSES * M], U8, name="w_plane", align_bytes=64)
+        nc.vector.quantize_mx(
+            out=w_codes[:].bitcast(FP8X4), scales=w_plane[:], in_=w_grouped[:].rearrange("p z m t -> p (z m t)")
+        )
+
+        def multiply(acc, z, codes, first, width):
+            nc.tensor.matmul_mx(
+                out=acc[:],
+                lhsT=w_codes[:, z * M : (z + 1) * M].bitcast(FP8X4),
+                lhsT_scale=w_plane[:, z * M : (z + 1) * M],
+                rhs=codes.bitcast(FP8X4),
+                rhs_scale=x_planes[ROWS * z :, first : first + width],
+                start=(z == 0),
+                stop=(z == PASSES - 1),
+            )
+
+        groups = [(0, 256), (256, 256), (512, 128), (640, 128)]
+        sums = {}
+        for first, width in groups:
+            sums[first] = psum.tile([M, width], F32, name="sums%d" % first)
+            multiply(sums[first], 0, x_codes0[:, first : first + width], first, width)
+
+        truth = keep.tile([M, S], F32, name="truth")
+        for g0 in range(0, S, GATHER):
+            x_codes1 = keep.tile([P, GATHER], U32, name="x_codes1_%d" % g0, align_bytes=64)
+            nc.vector.tensor_copy(
+                out=x_codes1[:],
+                in_=x_table[1][:].bitcast(U32).indirect(offsets[:, g0 // STRIPE : (g0 + GATHER) // STRIPE]),
+            )
+            for first, width in groups:
+                if g0 <= first < g0 + GATHER:
+                    multiply(sums[first], 1, x_codes1[:, first - g0 : first - g0 + width], first, width)
+                    nc.scalar.activation(out=truth[:, first : first + width], in_=sums[first][:], func=SIGMOID)
+        for v0 in range(0, V, BLOCK):
+            joined = keep.tile([M, BLOCK], F32, name="joined%d" % v0)
+            nc.vector.tensor_tensor(
+                out=joined[:],
+                in0=truth[:, v0 : v0 + BLOCK],
+                in1=truth[:, V + v0 : V + v0 + BLOCK],
+                op=mybir.AluOpType.mult,
+            )
+            nc.sync.dma_start(out=out[:, v0 : v0 + BLOCK], in_=joined[:])

@@ -33,7 +33,7 @@ def tile_picked_andpool_none_p_kernel(tc, x_words, x_scales, w1, offs, out):
         offsets = keep.tile([P, S // STRIPE], U16, name="offsets")
         x_table = [keep.tile([P, T], I32, name="x_table%d" % z) for z in range(PASSES)]
         scale_table = keep.tile([P, T], U8, name="scale_table")
-        w_raw = keep.tile([P, PASSES, PACK, M], F32, name="w_raw")
+        w_raw = [keep.tile([P, PACK, M], F32, name="w_raw%d" % z) for z in range(PASSES)]
 
         def load_words(z):
             nc.sync.dma_start(out=x_table[z][:], in_=x_words[z].rearrange("p c t -> p (c t)").bitcast(I32))
@@ -44,29 +44,27 @@ def tile_picked_andpool_none_p_kernel(tc, x_words, x_scales, w1, offs, out):
                 in_=x_scales[:, ROWS * q : ROWS * (q + 1), :].bitcast(I32),
             )
 
-        def load_w():
-            nc.sync.dma_start(out=w_raw[:], in_=w1.rearrange("(z p t) m -> p z t m", p=P, t=PACK))
+        def load_w(z):
+            rows = w1[z * P * PACK : (z + 1) * P * PACK, :]
+            nc.sync.dma_start(out=w_raw[z][:], in_=rows.rearrange("(p t) m -> p t m", t=PACK))
 
         nc.vector.memset(scale_table[:].bitcast(I32), 0)
+        load_w(0)
+        load_w(1)
         nc.sync.dma_start(offsets[:], offs)
-        load_words(0)
         for q in range(P // QUADRANT):
             load_scales(q, nc.sync)
-        load_w()
+        load_words(0)
         load_words(1)
 
-        warm_in = keep.tile([P, 1], F32, name="warm_in")
-        warm_out = keep.tile([P, 1], F32, name="warm_out")
-        nc.vector.memset(warm_in[:], 0.0)
-        nc.scalar.activation(out=warm_out[:], in_=warm_in[:], func=SIGMOID)
-
-        x_codes0 = keep.tile([P, S], U32, name="x_codes0", align_bytes=64)
-        nc.vector.tensor_copy(out=x_codes0[:], in_=x_table[0][:].bitcast(U32).indirect(offsets[:]))
         x_planes = keep.tile([P, S], U8, name="x_planes", align_bytes=64)
         nc.vector.tensor_copy(out=x_planes[:], in_=scale_table[:].indirect(offsets[:]))
+        x_codes0 = keep.tile([P, S], U32, name="x_codes0", align_bytes=64)
+        nc.vector.tensor_copy(out=x_codes0[:], in_=x_table[0][:].bitcast(U32).indirect(offsets[:]))
 
         w_grouped = keep.tile([P, PASSES, M, PACK], BF16, name="w_grouped", align_bytes=64)
-        nc.scalar.copy(out=w_grouped[:], in_=w_raw[:].rearrange("p z t m -> p z m t"))
+        for z in range(PASSES):
+            nc.scalar.copy(out=w_grouped[:, z], in_=w_raw[z][:].rearrange("p t m -> p m t"))
         w_codes = keep.tile([P, PASSES * M], U32, name="w_codes", align_bytes=64)
         w_plane = keep.tile([P, PASSES * M], U8, name="w_plane", align_bytes=64)
         nc.vector.quantize_mx(

@@ -19,9 +19,12 @@ PACK = 4
 PASSES = K // (P * PACK)
 QUADRANT = 32
 ROWS = 4
+PASS_BLOCKS = ROWS * P // QUADRANT
 STRIPE = 16
 GATHER = 256
 BLOCK = 128
+
+GROUPS = [(0, GATHER), (GATHER, GATHER), (2 * GATHER, BLOCK), (2 * GATHER + BLOCK, BLOCK)]
 
 
 def tile_picked_andpool_none_p_kernel(tc, x_words, x_scales, w1, offs, out):
@@ -35,32 +38,35 @@ def tile_picked_andpool_none_p_kernel(tc, x_words, x_scales, w1, offs, out):
         scale_table = keep.tile([P, T], U8, name="scale_table")
         w_raw = [keep.tile([P, PACK, M], F32, name="w_raw%d" % z) for z in range(PASSES)]
 
-        def load_words(z):
-            nc.sync.dma_start(out=x_table[z][:], in_=x_words[z].rearrange("p c t -> p (c t)").bitcast(I32))
+        nc.vector.memset(scale_table[:].bitcast(I32), 0)
 
-        def load_scales(q, queue):
-            queue.dma_start(
-                out=scale_table[QUADRANT * q : QUADRANT * q + PASSES * ROWS, :].bitcast(I32),
-                in_=x_scales[:, ROWS * q : ROWS * (q + 1), :].bitcast(I32),
-            )
-
-        def load_w(z):
+        for z in range(PASSES):
             rows = w1[z * P * PACK : (z + 1) * P * PACK, :]
             nc.sync.dma_start(out=w_raw[z][:], in_=rows.rearrange("(p t) m -> p t m", t=PACK))
-
-        nc.vector.memset(scale_table[:].bitcast(I32), 0)
-        load_w(0)
-        load_w(1)
         nc.sync.dma_start(offsets[:], offs)
-        for q in range(P // QUADRANT):
-            load_scales(q, nc.sync)
-        load_words(0)
-        load_words(1)
+        nc.sync.dma_start(
+            out=scale_table[0 : PASSES * PASS_BLOCKS, :].bitcast(I32),
+            in_=x_scales.rearrange("z b c -> (z b) c").bitcast(I32),
+        )
+        for z in range(PASSES):
+            nc.sync.dma_start(out=x_table[z][:], in_=x_words[z].rearrange("p c t -> p (c t)").bitcast(I32))
 
-        x_planes = keep.tile([P, S], U8, name="x_planes", align_bytes=64)
-        nc.vector.tensor_copy(out=x_planes[:], in_=scale_table[:].indirect(offsets[:]))
-        x_codes0 = keep.tile([P, S], U32, name="x_codes0", align_bytes=64)
-        nc.vector.tensor_copy(out=x_codes0[:], in_=x_table[0][:].bitcast(U32).indirect(offsets[:]))
+        picked_scales = keep.tile([P, S], U8, name="picked_scales")
+        nc.vector.tensor_copy(out=picked_scales[:], in_=scale_table[:].indirect(offsets[:]))
+        x_planes = [keep.tile([P, S], U8, name="x_plane%d" % z, align_bytes=64) for z in range(PASSES)]
+        for z in range(PASSES):
+            for q in range(P // QUADRANT):
+                block = PASS_BLOCKS * z + ROWS * q
+                plane_rows = x_planes[z][QUADRANT * q : QUADRANT * q + ROWS, :].bitcast(I32)
+                picked_rows = picked_scales[block : block + ROWS, :].bitcast(I32)
+                if block == QUADRANT * q:
+                    nc.vector.tensor_copy(out=plane_rows, in_=picked_rows)
+                else:
+                    queue = nc.sync if q % 2 else nc.scalar
+                    queue.dma_start(out=plane_rows, in_=picked_rows)
+
+        first_codes = keep.tile([P, S], U32, name="first_codes", align_bytes=64)
+        nc.vector.tensor_copy(out=first_codes[:], in_=x_table[0][:].bitcast(U32).indirect(offsets[:]))
 
         w_grouped = keep.tile([P, PASSES, M, PACK], BF16, name="w_grouped", align_bytes=64)
         for z in range(PASSES):
@@ -77,28 +83,28 @@ def tile_picked_andpool_none_p_kernel(tc, x_words, x_scales, w1, offs, out):
                 lhsT=w_codes[:, z * M : (z + 1) * M].bitcast(FP8X4),
                 lhsT_scale=w_plane[:, z * M : (z + 1) * M],
                 rhs=codes.bitcast(FP8X4),
-                rhs_scale=x_planes[ROWS * z :, first : first + width],
+                rhs_scale=x_planes[z][:, first : first + width],
                 start=(z == 0),
                 stop=(z == PASSES - 1),
             )
 
-        groups = [(0, 256), (256, 256), (512, 128), (640, 128)]
         sums = {}
-        for first, width in groups:
+        for first, width in GROUPS:
             sums[first] = psum.tile([M, width], F32, name="sums%d" % first)
-            multiply(sums[first], 0, x_codes0[:, first : first + width], first, width)
+            multiply(sums[first], 0, first_codes[:, first : first + width], first, width)
 
         truth = keep.tile([M, S], F32, name="truth")
         for g0 in range(0, S, GATHER):
-            x_codes1 = keep.tile([P, GATHER], U32, name="x_codes1_%d" % g0, align_bytes=64)
+            last_codes = keep.tile([P, GATHER], U32, name="last_codes%d" % g0, align_bytes=64)
             nc.vector.tensor_copy(
-                out=x_codes1[:],
+                out=last_codes[:],
                 in_=x_table[1][:].bitcast(U32).indirect(offsets[:, g0 // STRIPE : (g0 + GATHER) // STRIPE]),
             )
-            for first, width in groups:
+            for first, width in GROUPS:
                 if g0 <= first < g0 + GATHER:
-                    multiply(sums[first], 1, x_codes1[:, first - g0 : first - g0 + width], first, width)
+                    multiply(sums[first], 1, last_codes[:, first - g0 : first - g0 + width], first, width)
                     nc.scalar.activation(out=truth[:, first : first + width], in_=sums[first][:], func=SIGMOID)
+
         for v0 in range(0, V, BLOCK):
             joined = keep.tile([M, BLOCK], F32, name="joined%d" % v0)
             nc.vector.tensor_tensor(

@@ -38,18 +38,25 @@ def tile_picked_andpool_none_p_kernel(tc, x_words, x_scales, w1, offs, out):
         scale_table = keep.tile([P, T], U8, name="scale_table")
         w_raw = [keep.tile([P, PACK, M], F32, name="w_raw%d" % z) for z in range(PASSES)]
 
-        nc.vector.memset(scale_table[:].bitcast(I32), 0)
+        nc.vector.memset(scale_table[QUADRANT : 2 * QUADRANT, :].bitcast(I32), 0)
+        nc.vector.memset(scale_table[2 * QUADRANT :, :].bitcast(I32), 0)
 
-        for z in range(PASSES):
+        def load_weights(z):
             rows = w1[z * P * PACK : (z + 1) * P * PACK, :]
             nc.sync.dma_start(out=w_raw[z][:], in_=rows.rearrange("(p t) m -> p t m", t=PACK))
+
+        def load_words(z):
+            nc.sync.dma_start(out=x_table[z][:], in_=x_words[z].rearrange("p c t -> p (c t)").bitcast(I32))
+
+        load_weights(0)
         nc.sync.dma_start(offsets[:], offs)
         nc.sync.dma_start(
             out=scale_table[0 : PASSES * PASS_BLOCKS, :].bitcast(I32),
             in_=x_scales.rearrange("z b c -> (z b) c").bitcast(I32),
         )
-        for z in range(PASSES):
-            nc.sync.dma_start(out=x_table[z][:], in_=x_words[z].rearrange("p c t -> p (c t)").bitcast(I32))
+        load_words(0)
+        load_weights(1)
+        load_words(1)
 
         picked_scales = keep.tile([P, S], U8, name="picked_scales")
         nc.vector.tensor_copy(out=picked_scales[:], in_=scale_table[:].indirect(offsets[:]))
@@ -62,26 +69,27 @@ def tile_picked_andpool_none_p_kernel(tc, x_words, x_scales, w1, offs, out):
                 if block == QUADRANT * q:
                     nc.vector.tensor_copy(out=plane_rows, in_=picked_rows)
                 else:
-                    queue = nc.sync if q % 2 else nc.scalar
+                    queue = nc.sync if z else nc.scalar
                     queue.dma_start(out=plane_rows, in_=picked_rows)
 
         first_codes = keep.tile([P, S], U32, name="first_codes", align_bytes=64)
         nc.vector.tensor_copy(out=first_codes[:], in_=x_table[0][:].bitcast(U32).indirect(offsets[:]))
 
-        w_grouped = keep.tile([P, PASSES, M, PACK], BF16, name="w_grouped", align_bytes=64)
+        w_codes, w_planes = [], []
         for z in range(PASSES):
-            nc.scalar.copy(out=w_grouped[:, z], in_=w_raw[z][:].rearrange("p t m -> p m t"))
-        w_codes = keep.tile([P, PASSES * M], U32, name="w_codes", align_bytes=64)
-        w_plane = keep.tile([P, PASSES * M], U8, name="w_plane", align_bytes=64)
-        nc.vector.quantize_mx(
-            out=w_codes[:].bitcast(FP8X4), scales=w_plane[:], in_=w_grouped[:].rearrange("p z m t -> p (z m t)")
-        )
+            w_grouped = keep.tile([P, M, PACK], BF16, name="w_grouped%d" % z, align_bytes=64)
+            nc.scalar.copy(out=w_grouped[:], in_=w_raw[z][:].rearrange("p t m -> p m t"))
+            w_codes.append(keep.tile([P, M], U32, name="w_codes%d" % z, align_bytes=64))
+            w_planes.append(keep.tile([P, M], U8, name="w_plane%d" % z, align_bytes=64))
+            nc.vector.quantize_mx(
+                out=w_codes[z][:].bitcast(FP8X4), scales=w_planes[z][:], in_=w_grouped[:].rearrange("p m t -> p (m t)")
+            )
 
         def multiply(acc, z, codes, first, width):
             nc.tensor.matmul_mx(
                 out=acc[:],
-                lhsT=w_codes[:, z * M : (z + 1) * M].bitcast(FP8X4),
-                lhsT_scale=w_plane[:, z * M : (z + 1) * M],
+                lhsT=w_codes[z][:].bitcast(FP8X4),
+                lhsT_scale=w_planes[z][:],
                 rhs=codes.bitcast(FP8X4),
                 rhs_scale=x_planes[z][:, first : first + width],
                 start=(z == 0),

@@ -24,7 +24,7 @@ STRIPE = 16
 GATHER = 256
 BLOCK = 128
 
-GROUPS = [(0, GATHER), (GATHER, GATHER), (2 * GATHER, BLOCK), (2 * GATHER + BLOCK, BLOCK)]
+GROUPS = [(0, 128), (128, 128), (256, 256), (512, 128), (640, 128)]
 
 
 def tile_picked_andpool_none_p_kernel(tc, x_words, x_scales, w1, offs, out):
@@ -35,33 +35,32 @@ def tile_picked_andpool_none_p_kernel(tc, x_words, x_scales, w1, offs, out):
 
         offsets = keep.tile([P, S // STRIPE], U16, name="offsets")
         x_table = [keep.tile([P, T], I32, name="x_table%d" % z) for z in range(PASSES)]
-        scale_table = keep.tile([P, T], U8, name="scale_table")
-        w_raw = [keep.tile([P, PACK, M], F32, name="w_raw%d" % z) for z in range(PASSES)]
+        scale_table = keep.tile([P, T], U8, name="scale_table", tag="scales_then_weights", align_bytes=64)
+
+        warm_in = keep.tile([P, 1], F32, name="warm_in")
+        warm_out = keep.tile([P, 1], F32, name="warm_out")
+        nc.vector.memset(warm_in[:], 0.0)
+        nc.scalar.activation(out=warm_out[:], in_=warm_in[:], func=SIGMOID)
 
         nc.vector.memset(scale_table[QUADRANT : 2 * QUADRANT, :].bitcast(I32), 0)
         nc.vector.memset(scale_table[2 * QUADRANT :, :].bitcast(I32), 0)
 
-        def load_weights(z):
-            rows = w1[z * P * PACK : (z + 1) * P * PACK, :]
-            nc.sync.dma_start(out=w_raw[z][:], in_=rows.rearrange("(p t) m -> p t m", t=PACK))
-
-        def load_words(z):
-            nc.sync.dma_start(out=x_table[z][:], in_=x_words[z].rearrange("p c t -> p (c t)").bitcast(I32))
-
-        load_weights(0)
+        w_rows = [w1[z * P * PACK : (z + 1) * P * PACK, :].rearrange("(p t) m -> p t m", t=PACK) for z in range(PASSES)]
+        w_first = keep.tile([P, PACK, M], F32, name="w_first")
         nc.sync.dma_start(offsets[:], offs)
         nc.sync.dma_start(
             out=scale_table[0 : PASSES * PASS_BLOCKS, :].bitcast(I32),
             in_=x_scales.rearrange("z b c -> (z b) c").bitcast(I32),
         )
-        load_words(0)
-        load_weights(1)
-        load_words(1)
+        nc.sync.dma_start(out=w_first[:], in_=w_rows[0])
+        for z in range(PASSES):
+            nc.sync.dma_start(out=x_table[z][:], in_=x_words[z].rearrange("p c t -> p (c t)").bitcast(I32))
 
         picked_scales = keep.tile([P, S], U8, name="picked_scales")
         nc.vector.tensor_copy(out=picked_scales[:], in_=scale_table[:].indirect(offsets[:]))
         x_planes = [keep.tile([P, S], U8, name="x_plane%d" % z, align_bytes=64) for z in range(PASSES)]
-        for z in range(PASSES):
+
+        def move_scales(z):
             for q in range(P // QUADRANT):
                 block = PASS_BLOCKS * z + ROWS * q
                 plane_rows = x_planes[z][QUADRANT * q : QUADRANT * q + ROWS, :].bitcast(I32)
@@ -69,8 +68,12 @@ def tile_picked_andpool_none_p_kernel(tc, x_words, x_scales, w1, offs, out):
                 if block == QUADRANT * q:
                     nc.vector.tensor_copy(out=plane_rows, in_=picked_rows)
                 else:
-                    queue = nc.sync if z else nc.scalar
-                    queue.dma_start(out=plane_rows, in_=picked_rows)
+                    nc.sync.dma_start(out=plane_rows, in_=picked_rows)
+
+        move_scales(0)
+        w_last = keep.tile([P, PACK, M], F32, name="w_last", tag="scales_then_weights", align_bytes=64)
+        nc.sync.dma_start(out=w_last[:], in_=w_rows[1])
+        move_scales(1)
 
         first_codes = keep.tile([P, S], U32, name="first_codes", align_bytes=64)
         nc.vector.tensor_copy(out=first_codes[:], in_=x_table[0][:].bitcast(U32).indirect(offsets[:]))
@@ -78,7 +81,10 @@ def tile_picked_andpool_none_p_kernel(tc, x_words, x_scales, w1, offs, out):
         w_codes, w_planes = [], []
         for z in range(PASSES):
             w_grouped = keep.tile([P, M, PACK], BF16, name="w_grouped%d" % z, align_bytes=64)
-            nc.scalar.copy(out=w_grouped[:], in_=w_raw[z][:].rearrange("p t m -> p m t"))
+            nc.scalar.copy(
+                out=w_grouped[:].rearrange("p (c i) t -> p c t i", i=PACK),
+                in_=(w_first, w_last)[z][:].rearrange("p t (c i) -> p c t i", i=PACK),
+            )
             w_codes.append(keep.tile([P, M], U32, name="w_codes%d" % z, align_bytes=64))
             w_planes.append(keep.tile([P, M], U8, name="w_plane%d" % z, align_bytes=64))
             nc.vector.quantize_mx(
@@ -103,7 +109,8 @@ def tile_picked_andpool_none_p_kernel(tc, x_words, x_scales, w1, offs, out):
 
         truth = keep.tile([M, S], F32, name="truth")
         for g0 in range(0, S, GATHER):
-            last_codes = keep.tile([P, GATHER], U32, name="last_codes%d" % g0, align_bytes=64)
+            tag = "scales_then_weights" if g0 == 512 else "last_codes%d" % g0
+            last_codes = keep.tile([P, GATHER], U32, name="last_codes%d" % g0, tag=tag, align_bytes=64)
             nc.vector.tensor_copy(
                 out=last_codes[:],
                 in_=x_table[1][:].bitcast(U32).indirect(offsets[:, g0 // STRIPE : (g0 + GATHER) // STRIPE]),

@@ -48,7 +48,7 @@ def tile_picked_andpool_none_p_kernel(tc, x_words, x_scales, w1, offs, out):
         w_rows = [w1[z * P * PACK : (z + 1) * P * PACK, :].rearrange("(p t) m -> p t m", t=PACK) for z in range(PASSES)]
         w_first = keep.tile([P, PACK, M], F32, name="w_first")
         nc.sync.dma_start(offsets[:], offs)
-        nc.sync.dma_start(
+        nc.scalar.dma_start(
             out=scale_table[0 : PASSES * PASS_BLOCKS, :].bitcast(I32),
             in_=x_scales.rearrange("z b c -> (z b) c").bitcast(I32),
         )
@@ -68,7 +68,8 @@ def tile_picked_andpool_none_p_kernel(tc, x_words, x_scales, w1, offs, out):
                 if block == QUADRANT * q:
                     nc.vector.tensor_copy(out=plane_rows, in_=picked_rows)
                 else:
-                    nc.sync.dma_start(out=plane_rows, in_=picked_rows)
+                    queue = nc.gpsimd if z == 1 and q < 1 else nc.sync
+                    queue.dma_start(out=plane_rows, in_=picked_rows)
 
         move_scales(0)
         w_last = keep.tile([P, PACK, M], F32, name="w_last", tag="scales_then_weights", align_bytes=64)
@@ -128,4 +129,5 @@ def tile_picked_andpool_none_p_kernel(tc, x_words, x_scales, w1, offs, out):
                 in1=truth[:, V + v0 : V + v0 + BLOCK],
                 op=mybir.AluOpType.mult,
             )
-            nc.sync.dma_start(out=out[:, v0 : v0 + BLOCK], in_=joined[:])
+            queue = nc.scalar if v0 == BLOCK else nc.sync
+            queue.dma_start(out=out[:, v0 : v0 + BLOCK], in_=joined[:])

@@ -12,7 +12,7 @@ U32 = mybir.dt.uint32
 U16 = mybir.dt.uint16
 U8 = mybir.dt.uint8
 FP8X4 = mybir.dt.float8_e4m3fn_x4
-SIGMOID = mybir.ActivationFunctionType.Sigmoid
+TANH = mybir.ActivationFunctionType.Tanh
 
 P = 128
 PACK = 4
@@ -24,6 +24,8 @@ STRIPE = 16
 GATHER = 256
 BLOCK = 128
 
+EARLY = 1
+SHIFT = 12
 GROUPS = [(0, 128), (128, 128), (256, 256), (512, 128), (640, 128)]
 
 
@@ -35,46 +37,40 @@ def tile_picked_andpool_none_p_kernel(tc, x_words, x_scales, w1, offs, out):
 
         offsets = keep.tile([P, S // STRIPE], U16, name="offsets")
         x_table = [keep.tile([P, T], I32, name="x_table%d" % z) for z in range(PASSES)]
-        scale_table = keep.tile([P, T], U8, name="scale_table", tag="scales_then_weights", align_bytes=64)
+        scale_table = keep.tile([P, T], U8, name="scale_table")
 
-        warm_in = keep.tile([P, 1], F32, name="warm_in")
-        warm_out = keep.tile([P, 1], F32, name="warm_out")
-        nc.vector.memset(warm_in[:], 0.0)
-        nc.scalar.activation(out=warm_out[:], in_=warm_in[:], func=SIGMOID)
-
-        nc.vector.memset(scale_table[QUADRANT : 2 * QUADRANT, :].bitcast(I32), 0)
-        nc.vector.memset(scale_table[2 * QUADRANT :, :].bitcast(I32), 0)
+        nc.vector.memset(scale_table[:].bitcast(I32), 0)
 
         w_rows = [w1[z * P * PACK : (z + 1) * P * PACK, :].rearrange("(p t) m -> p t m", t=PACK) for z in range(PASSES)]
         w_first = keep.tile([P, PACK, M], F32, name="w_first")
+        w_early = keep.tile([P, EARLY, M], F32, name="w_early")
+        w_last = keep.tile([P, PACK - EARLY, M], F32, name="w_last", align_bytes=64)
+        nc.sync.dma_start(out=w_first[:], in_=w_rows[0])
         nc.sync.dma_start(offsets[:], offs)
-        nc.scalar.dma_start(
-            out=scale_table[0 : PASSES * PASS_BLOCKS, :].bitcast(I32),
+        nc.sync.dma_start(out=w_early[:], in_=w_rows[1][:, :EARLY])
+        nc.sync.dma_start(
+            out=scale_table[SHIFT : SHIFT + PASSES * PASS_BLOCKS, :].bitcast(I32),
             in_=x_scales.rearrange("z b c -> (z b) c").bitcast(I32),
         )
-        nc.sync.dma_start(out=w_first[:], in_=w_rows[0])
         for z in range(PASSES):
             nc.sync.dma_start(out=x_table[z][:], in_=x_words[z].rearrange("p c t -> p (c t)").bitcast(I32))
+        nc.sync.dma_start(out=w_last[:], in_=w_rows[1][:, EARLY:])
 
         picked_scales = keep.tile([P, S], U8, name="picked_scales")
         nc.vector.tensor_copy(out=picked_scales[:], in_=scale_table[:].indirect(offsets[:]))
-        x_planes = [keep.tile([P, S], U8, name="x_plane%d" % z, align_bytes=64) for z in range(PASSES)]
+        x_planes = keep.tile([P, S], U8, name="x_planes", align_bytes=64)
+        in_place = slice(0, QUADRANT + ROWS)
+        nc.vector.tensor_copy(out=x_planes[in_place, :].bitcast(I32), in_=picked_scales[in_place, :].bitcast(I32))
 
-        def move_scales(z):
+        plane_start = (SHIFT, 0)
+        for z in range(PASSES):
             for q in range(P // QUADRANT):
-                block = PASS_BLOCKS * z + ROWS * q
-                plane_rows = x_planes[z][QUADRANT * q : QUADRANT * q + ROWS, :].bitcast(I32)
-                picked_rows = picked_scales[block : block + ROWS, :].bitcast(I32)
-                if block == QUADRANT * q:
-                    nc.vector.tensor_copy(out=plane_rows, in_=picked_rows)
-                else:
-                    queue = nc.gpsimd if z == 1 and q < 1 else nc.sync
-                    queue.dma_start(out=plane_rows, in_=picked_rows)
-
-        move_scales(0)
-        w_last = keep.tile([P, PACK, M], F32, name="w_last", tag="scales_then_weights", align_bytes=64)
-        nc.sync.dma_start(out=w_last[:], in_=w_rows[1])
-        move_scales(1)
+                at = SHIFT + PASS_BLOCKS * z + ROWS * q
+                to = QUADRANT * q + plane_start[z]
+                if at != to:
+                    nc.sync.dma_start(
+                        out=x_planes[to : to + ROWS, :].bitcast(I32), in_=picked_scales[at : at + ROWS, :].bitcast(I32)
+                    )
 
         first_codes = keep.tile([P, S], U32, name="first_codes", align_bytes=64)
         nc.vector.tensor_copy(out=first_codes[:], in_=x_table[0][:].bitcast(U32).indirect(offsets[:]))
@@ -82,10 +78,9 @@ def tile_picked_andpool_none_p_kernel(tc, x_words, x_scales, w1, offs, out):
         w_codes, w_planes = [], []
         for z in range(PASSES):
             w_grouped = keep.tile([P, M, PACK], BF16, name="w_grouped%d" % z, align_bytes=64)
-            nc.scalar.copy(
-                out=w_grouped[:].rearrange("p (c i) t -> p c t i", i=PACK),
-                in_=(w_first, w_last)[z][:].rearrange("p t (c i) -> p c t i", i=PACK),
-            )
+            parts = ((0, PACK, w_first),) if z == 0 else ((0, EARLY, w_early), (EARLY, PACK, w_last))
+            for t0, t1, raw in parts:
+                nc.scalar.copy(out=w_grouped[:, :, t0:t1], in_=raw[:].rearrange("p t m -> p m t"))
             w_codes.append(keep.tile([P, M], U32, name="w_codes%d" % z, align_bytes=64))
             w_planes.append(keep.tile([P, M], U8, name="w_plane%d" % z, align_bytes=64))
             nc.vector.quantize_mx(
@@ -98,7 +93,7 @@ def tile_picked_andpool_none_p_kernel(tc, x_words, x_scales, w1, offs, out):
                 lhsT=w_codes[z][:].bitcast(FP8X4),
                 lhsT_scale=w_planes[z][:],
                 rhs=codes.bitcast(FP8X4),
-                rhs_scale=x_planes[z][:, first : first + width],
+                rhs_scale=x_planes[plane_start[z] :, first : first + width],
                 start=(z == 0),
                 stop=(z == PASSES - 1),
             )
@@ -110,7 +105,7 @@ def tile_picked_andpool_none_p_kernel(tc, x_words, x_scales, w1, offs, out):
 
         truth = keep.tile([M, S], F32, name="truth")
         for g0 in range(0, S, GATHER):
-            tag = "scales_then_weights" if g0 == 512 else "last_codes%d" % g0
+            tag = "w_last" if g0 == 512 else "last_codes%d" % g0
             last_codes = keep.tile([P, GATHER], U32, name="last_codes%d" % g0, tag=tag, align_bytes=64)
             nc.vector.tensor_copy(
                 out=last_codes[:],
@@ -119,15 +114,22 @@ def tile_picked_andpool_none_p_kernel(tc, x_words, x_scales, w1, offs, out):
             for first, width in GROUPS:
                 if g0 <= first < g0 + GATHER:
                     multiply(sums[first], 1, last_codes[:, first - g0 : first - g0 + width], first, width)
-                    nc.scalar.activation(out=truth[:, first : first + width], in_=sums[first][:], func=SIGMOID)
+                    nc.scalar.activation(out=truth[:, first : first + width], in_=sums[first][:], func=TANH, scale=0.5)
 
+        quarter = keep.tile([M, V], F32, name="quarter")
+        for c0, c1 in ((0, GATHER), (GATHER, V)):
+            nc.vector.tensor_scalar(
+                out=quarter[:, c0:c1], in0=truth[:, c0:c1], scalar1=1.0, scalar2=0.25,
+                op0=mybir.AluOpType.add, op1=mybir.AluOpType.mult,
+            )
         for v0 in range(0, V, BLOCK):
             joined = keep.tile([M, BLOCK], F32, name="joined%d" % v0)
-            nc.vector.tensor_tensor(
+            nc.vector.scalar_tensor_tensor(
                 out=joined[:],
-                in0=truth[:, v0 : v0 + BLOCK],
-                in1=truth[:, V + v0 : V + v0 + BLOCK],
-                op=mybir.AluOpType.mult,
+                in0=truth[:, V + v0 : V + v0 + BLOCK],
+                scalar=1.0,
+                in1=quarter[:, v0 : v0 + BLOCK],
+                op0=mybir.AluOpType.add,
+                op1=mybir.AluOpType.mult,
             )
-            queue = nc.scalar if v0 == BLOCK else nc.sync
-            queue.dma_start(out=out[:, v0 : v0 + BLOCK], in_=joined[:])
+            nc.sync.dma_start(out=out[:, v0 : v0 + BLOCK], in_=joined[:])

@@ -26,7 +26,7 @@ BLOCK = 128
 
 EARLY = 1
 SHIFT = 12
-GROUPS = [(0, 128), (128, 128), (256, 256), (512, 128), (640, 128)]
+GROUPS = [(first, BLOCK) for first in range(0, S, BLOCK)]
 
 
 def tile_picked_andpool_none_p_kernel(tc, x_words, x_scales, w1, offs, out):
@@ -117,7 +117,7 @@ def tile_picked_andpool_none_p_kernel(tc, x_words, x_scales, w1, offs, out):
                     nc.scalar.activation(out=truth[:, first : first + width], in_=sums[first][:], func=TANH, scale=0.5)
 
         quarter = keep.tile([M, V], F32, name="quarter")
-        for c0, c1 in ((0, GATHER), (GATHER, V)):
+        for c0, c1 in ((0, BLOCK), (BLOCK, 2 * BLOCK), (2 * BLOCK, V)):
             nc.vector.tensor_scalar(
                 out=quarter[:, c0:c1], in0=truth[:, c0:c1], scalar1=1.0, scalar2=0.25,
                 op0=mybir.AluOpType.add, op1=mybir.AluOpType.mult,

@@ -80,7 +80,10 @@ def tile_picked_andpool_none_p_kernel(tc, x_words, x_scales, w1, offs, out):
             w_grouped = keep.tile([P, M, PACK], BF16, name="w_grouped%d" % z, align_bytes=64)
             parts = ((0, PACK, w_first),) if z == 0 else ((0, EARLY, w_early), (EARLY, PACK, w_last))
             for t0, t1, raw in parts:
-                nc.scalar.copy(out=w_grouped[:, :, t0:t1], in_=raw[:].rearrange("p t m -> p m t"))
+                nc.scalar.copy(
+                    out=w_grouped[:, :, t0:t1].rearrange("p (c i) t -> p c t i", i=PACK),
+                    in_=raw[:].rearrange("p t (c i) -> p c t i", i=PACK),
+                )
             w_codes.append(keep.tile([P, M], U32, name="w_codes%d" % z, align_bytes=64))
             w_planes.append(keep.tile([P, M], U8, name="w_plane%d" % z, align_bytes=64))
             nc.vector.quantize_mx(

@@ -25,7 +25,7 @@ GATHER = 256
 BLOCK = 128
 
 EARLY = 1
-SHIFT = 12
+SPREAD = 4
 GROUPS = [(first, BLOCK) for first in range(0, S, BLOCK)]
 
 
@@ -49,8 +49,8 @@ def tile_picked_andpool_none_p_kernel(tc, x_words, x_scales, w1, offs, out):
         nc.sync.dma_start(offsets[:], offs)
         nc.sync.dma_start(out=w_early[:], in_=w_rows[1][:, :EARLY])
         nc.sync.dma_start(
-            out=scale_table[SHIFT : SHIFT + PASSES * PASS_BLOCKS, :].bitcast(I32),
-            in_=x_scales.rearrange("z b c -> (z b) c").bitcast(I32),
+            out=scale_table[::SPREAD, :].bitcast(I32),
+            in_=x_scales.rearrange("z b c -> b z c").bitcast(I32),
         )
         for z in range(PASSES):
             nc.sync.dma_start(out=x_table[z][:], in_=x_words[z].rearrange("p c t -> p (c t)").bitcast(I32))
@@ -59,18 +59,16 @@ def tile_picked_andpool_none_p_kernel(tc, x_words, x_scales, w1, offs, out):
         picked_scales = keep.tile([P, S], U8, name="picked_scales")
         nc.vector.tensor_copy(out=picked_scales[:], in_=scale_table[:].indirect(offsets[:]))
         x_planes = keep.tile([P, S], U8, name="x_planes", align_bytes=64)
-        in_place = slice(0, QUADRANT + ROWS)
-        nc.vector.tensor_copy(out=x_planes[in_place, :].bitcast(I32), in_=picked_scales[in_place, :].bitcast(I32))
+        nc.vector.tensor_copy(out=x_planes[:].bitcast(I32), in_=picked_scales[:].bitcast(I32))
 
-        plane_start = (SHIFT, 0)
+        plane_start = (0, SPREAD)
         for z in range(PASSES):
-            for q in range(P // QUADRANT):
-                at = SHIFT + PASS_BLOCKS * z + ROWS * q
-                to = QUADRANT * q + plane_start[z]
-                if at != to:
-                    nc.sync.dma_start(
-                        out=x_planes[to : to + ROWS, :].bitcast(I32), in_=picked_scales[at : at + ROWS, :].bitcast(I32)
-                    )
+            for r in range(1, ROWS):
+                at = SPREAD * (PASSES * r + z)
+                to = plane_start[z] + r
+                nc.sync.dma_start(
+                    out=x_planes[to::QUADRANT, :].bitcast(I32), in_=picked_scales[at::QUADRANT, :].bitcast(I32)
+                )
 
         first_codes = keep.tile([P, S], U32, name="first_codes", align_bytes=64)
         nc.vector.tensor_copy(out=first_codes[:], in_=x_table[0][:].bitcast(U32).indirect(offsets[:]))

@@ -58,8 +58,11 @@ def tile_picked_andpool_none_p_kernel(tc, x_words, x_scales, w1, offs, out):
 
         picked_scales = keep.tile([P, S], U8, name="picked_scales")
         nc.vector.tensor_copy(out=picked_scales[:], in_=scale_table[:].indirect(offsets[:]))
-        x_planes = keep.tile([P, S], U8, name="x_planes", align_bytes=64)
-        nc.vector.tensor_copy(out=x_planes[:].bitcast(I32), in_=picked_scales[:].bitcast(I32))
+        x_planes = keep.tile([P, PASSES * S], U8, name="x_planes", align_bytes=64)
+        nc.vector.tensor_copy(
+            out=x_planes[:].bitcast(I32).rearrange("p (z c) -> p z c", z=PASSES),
+            in_=picked_scales[:].bitcast(I32).unsqueeze(1).to_broadcast([P, PASSES, S // PACK]),
+        )
 
         plane_start = (0, SPREAD)
         for z in range(PASSES):
@@ -67,7 +70,8 @@ def tile_picked_andpool_none_p_kernel(tc, x_words, x_scales, w1, offs, out):
                 at = SPREAD * (PASSES * r + z)
                 to = plane_start[z] + r
                 nc.sync.dma_start(
-                    out=x_planes[to::QUADRANT, :].bitcast(I32), in_=picked_scales[at::QUADRANT, :].bitcast(I32)
+                    out=x_planes[to::QUADRANT, z * S : (z + 1) * S].bitcast(I32),
+                    in_=picked_scales[at::QUADRANT, :].bitcast(I32),
                 )
 
         first_codes = keep.tile([P, S], U32, name="first_codes", align_bytes=64)
@@ -94,7 +98,7 @@ def tile_picked_andpool_none_p_kernel(tc, x_words, x_scales, w1, offs, out):
                 lhsT=w_codes[z][:].bitcast(FP8X4),
                 lhsT_scale=w_planes[z][:],
                 rhs=codes.bitcast(FP8X4),
-                rhs_scale=x_planes[plane_start[z] :, first : first + width],
+                rhs_scale=x_planes[plane_start[z] :, z * S + first : z * S + first + width],
                 start=(z == 0),
                 stop=(z == PASSES - 1),
             )
@@ -105,15 +109,15 @@ def tile_picked_andpool_none_p_kernel(tc, x_words, x_scales, w1, offs, out):
             multiply(sums[first], 0, first_codes[:, first : first + width], first, width)
 
         truth = keep.tile([M, S], F32, name="truth")
-        for g0 in range(0, S, GATHER):
-            tag = "w_last" if g0 == 512 else "last_codes%d" % g0
-            last_codes = keep.tile([P, GATHER], U32, name="last_codes%d" % g0, tag=tag, align_bytes=64)
+        for g0, g1 in ((0, S - GATHER), (S - GATHER, S)):
+            tag = "w_last" if g1 == S else "last_codes%d" % g0
+            last_codes = keep.tile([P, g1 - g0], U32, name="last_codes%d" % g0, tag=tag, align_bytes=64)
             nc.vector.tensor_copy(
                 out=last_codes[:],
-                in_=x_table[1][:].bitcast(U32).indirect(offsets[:, g0 // STRIPE : (g0 + GATHER) // STRIPE]),
+                in_=x_table[1][:].bitcast(U32).indirect(offsets[:, g0 // STRIPE : g1 // STRIPE]),
             )
             for first, width in GROUPS:
-                if g0 <= first < g0 + GATHER:
+                if g0 <= first < g1:
                     multiply(sums[first], 1, last_codes[:, first - g0 : first - g0 + width], first, width)
                     nc.scalar.activation(out=truth[:, first : first + width], in_=sums[first][:], func=TANH, scale=0.5)
 

@@ -12,7 +12,7 @@ U32 = mybir.dt.uint32
 U16 = mybir.dt.uint16
 U8 = mybir.dt.uint8
 FP8X4 = mybir.dt.float8_e4m3fn_x4
-TANH = mybir.ActivationFunctionType.Tanh
+SIGMOID = mybir.ActivationFunctionType.Sigmoid
 
 P = 128
 PACK = 4
@@ -37,7 +37,7 @@ def tile_picked_andpool_none_p_kernel(tc, x_words, x_scales, w1, offs, out):
 
         offsets = keep.tile([P, S // STRIPE], U16, name="offsets")
         x_table = [keep.tile([P, T], I32, name="x_table%d" % z) for z in range(PASSES)]
-        scale_table = keep.tile([P, T], U8, name="scale_table")
+        scale_table = keep.tile([P, T], U8, name="scale_table", align_bytes=64)
 
         nc.vector.memset(scale_table[:].bitcast(I32), 0)
 
@@ -56,13 +56,14 @@ def tile_picked_andpool_none_p_kernel(tc, x_words, x_scales, w1, offs, out):
             nc.sync.dma_start(out=x_table[z][:], in_=x_words[z].rearrange("p c t -> p (c t)").bitcast(I32))
         nc.sync.dma_start(out=w_last[:], in_=w_rows[1][:, EARLY:])
 
+        warm = keep.tile([P, 2], F32, name="warm")
+        nc.gpsimd.memset(warm[:, 0:1], 0.0)
+        nc.scalar.activation(out=warm[:, 1:2], in_=warm[:, 0:1], func=SIGMOID)
+
         picked_scales = keep.tile([P, S], U8, name="picked_scales")
         nc.vector.tensor_copy(out=picked_scales[:], in_=scale_table[:].indirect(offsets[:]))
-        x_planes = keep.tile([P, PASSES * S], U8, name="x_planes", align_bytes=64)
-        nc.vector.tensor_copy(
-            out=x_planes[:].bitcast(I32).rearrange("p (z c) -> p z c", z=PASSES),
-            in_=picked_scales[:].bitcast(I32).unsqueeze(1).to_broadcast([P, PASSES, S // PACK]),
-        )
+        x_planes = keep.tile([P, S], U8, name="x_planes", align_bytes=64)
+        nc.vector.tensor_copy(out=x_planes[:].bitcast(I32), in_=picked_scales[:].bitcast(I32))
 
         plane_start = (0, SPREAD)
         for z in range(PASSES):
@@ -70,7 +71,7 @@ def tile_picked_andpool_none_p_kernel(tc, x_words, x_scales, w1, offs, out):
                 at = SPREAD * (PASSES * r + z)
                 to = plane_start[z] + r
                 nc.sync.dma_start(
-                    out=x_planes[to::QUADRANT, z * S : (z + 1) * S].bitcast(I32),
+                    out=x_planes[to::QUADRANT, :].bitcast(I32),
                     in_=picked_scales[at::QUADRANT, :].bitcast(I32),
                 )
 
@@ -86,7 +87,8 @@ def tile_picked_andpool_none_p_kernel(tc, x_words, x_scales, w1, offs, out):
                     out=w_grouped[:, :, t0:t1].rearrange("p (c i) t -> p c t i", i=PACK),
                     in_=raw[:].rearrange("p t (c i) -> p c t i", i=PACK),
                 )
-            w_codes.append(keep.tile([P, M], U32, name="w_codes%d" % z, align_bytes=64))
+            tag = "scale_table" if z == 0 else "w_codes"
+            w_codes.append(keep.tile([P, M], U32, name="w_codes%d" % z, tag=tag, align_bytes=64))
             w_planes.append(keep.tile([P, M], U8, name="w_plane%d" % z, align_bytes=64))
             nc.vector.quantize_mx(
                 out=w_codes[z][:].bitcast(FP8X4), scales=w_planes[z][:], in_=w_grouped[:].rearrange("p m t -> p (m t)")
@@ -98,7 +100,7 @@ def tile_picked_andpool_none_p_kernel(tc, x_words, x_scales, w1, offs, out):
                 lhsT=w_codes[z][:].bitcast(FP8X4),
                 lhsT_scale=w_planes[z][:],
                 rhs=codes.bitcast(FP8X4),
-                rhs_scale=x_planes[plane_start[z] :, z * S + first : z * S + first + width],
+                rhs_scale=x_planes[plane_start[z] :, first : first + width],
                 start=(z == 0),
                 stop=(z == PASSES - 1),
             )
@@ -108,33 +110,32 @@ def tile_picked_andpool_none_p_kernel(tc, x_words, x_scales, w1, offs, out):
             sums[first] = psum.tile([M, width], F32, name="sums%d" % first)
             multiply(sums[first], 0, first_codes[:, first : first + width], first, width)
 
-        truth = keep.tile([M, S], F32, name="truth")
+        last_codes = {}
         for g0, g1 in ((0, S - GATHER), (S - GATHER, S)):
             tag = "w_last" if g1 == S else "last_codes%d" % g0
-            last_codes = keep.tile([P, g1 - g0], U32, name="last_codes%d" % g0, tag=tag, align_bytes=64)
+            picked = keep.tile([P, g1 - g0], U32, name="last_codes%d" % g0, tag=tag, align_bytes=64)
             nc.vector.tensor_copy(
-                out=last_codes[:],
-                in_=x_table[1][:].bitcast(U32).indirect(offsets[:, g0 // STRIPE : g1 // STRIPE]),
+                out=picked[:], in_=x_table[1][:].bitcast(U32).indirect(offsets[:, g0 // STRIPE : g1 // STRIPE])
             )
-            for first, width in GROUPS:
-                if g0 <= first < g1:
-                    multiply(sums[first], 1, last_codes[:, first - g0 : first - g0 + width], first, width)
-                    nc.scalar.activation(out=truth[:, first : first + width], in_=sums[first][:], func=TANH, scale=0.5)
+            for first in range(g0, g1, BLOCK):
+                last_codes[first] = picked[:, first - g0 : first - g0 + BLOCK]
 
-        quarter = keep.tile([M, V], F32, name="quarter")
-        for c0, c1 in ((0, BLOCK), (BLOCK, 2 * BLOCK), (2 * BLOCK, V)):
-            nc.vector.tensor_scalar(
-                out=quarter[:, c0:c1], in0=truth[:, c0:c1], scalar1=1.0, scalar2=0.25,
-                op0=mybir.AluOpType.add, op1=mybir.AluOpType.mult,
-            )
+        truth = keep.tile([M, S], F32, name="truth")
+        last = S - BLOCK
+        for first in (0, V, BLOCK, 2 * BLOCK, V + BLOCK, last):
+            multiply(sums[first], 1, last_codes[first], first, BLOCK)
+            step = BLOCK // 2 if first == last else BLOCK
+            for c0 in range(0, BLOCK, step):
+                nc.scalar.activation(
+                    out=truth[:, first + c0 : first + c0 + step], in_=sums[first][:, c0 : c0 + step], func=SIGMOID
+                )
         for v0 in range(0, V, BLOCK):
             joined = keep.tile([M, BLOCK], F32, name="joined%d" % v0)
-            nc.vector.scalar_tensor_tensor(
-                out=joined[:],
-                in0=truth[:, V + v0 : V + v0 + BLOCK],
-                scalar=1.0,
-                in1=quarter[:, v0 : v0 + BLOCK],
-                op0=mybir.AluOpType.add,
-                op1=mybir.AluOpType.mult,
-            )
+            step = BLOCK // 2 if V + v0 == last else BLOCK
+            for c0 in range(0, BLOCK, step):
+                nc.vector.tensor_mul(
+                    out=joined[:, c0 : c0 + step],
+                    in0=truth[:, v0 + c0 : v0 + c0 + step],
+                    in1=truth[:, V + v0 + c0 : V + v0 + c0 + step],
+                )
             nc.sync.dma_start(out=out[:, v0 : v0 + BLOCK], in_=joined[:])

@@ -24,7 +24,8 @@ STRIPE = 16
 GATHER = 256
 BLOCK = 128
 
-EARLY = 1
+HEAD = T // 8
+SCALAR_SHARE = 72
 SPREAD = 4
 GROUPS = [(first, BLOCK) for first in range(0, S, BLOCK)]
 
@@ -43,18 +44,18 @@ def tile_picked_andpool_none_p_kernel(tc, x_words, x_scales, w1, offs, out):
 
         w_rows = [w1[z * P * PACK : (z + 1) * P * PACK, :].rearrange("(p t) m -> p t m", t=PACK) for z in range(PASSES)]
         w_first = keep.tile([P, PACK, M], F32, name="w_first")
-        w_early = keep.tile([P, EARLY, M], F32, name="w_early")
-        w_last = keep.tile([P, PACK - EARLY, M], F32, name="w_last", align_bytes=64)
+        w_last = keep.tile([P, PACK, M], F32, name="w_last", align_bytes=64)
+        x_rows = [x_words[z].rearrange("p c t -> p (c t)").bitcast(I32) for z in range(PASSES)]
         nc.sync.dma_start(out=w_first[:], in_=w_rows[0])
         nc.sync.dma_start(offsets[:], offs)
-        nc.sync.dma_start(out=w_early[:], in_=w_rows[1][:, :EARLY])
+        nc.sync.dma_start(out=x_table[0][:, :HEAD], in_=x_rows[0][:, :HEAD])
         nc.sync.dma_start(
             out=scale_table[::SPREAD, :].bitcast(I32),
             in_=x_scales.rearrange("z b c -> b z c").bitcast(I32),
         )
-        for z in range(PASSES):
-            nc.sync.dma_start(out=x_table[z][:], in_=x_words[z].rearrange("p c t -> p (c t)").bitcast(I32))
-        nc.sync.dma_start(out=w_last[:], in_=w_rows[1][:, EARLY:])
+        nc.sync.dma_start(out=x_table[0][:, HEAD:], in_=x_rows[0][:, HEAD:])
+        nc.sync.dma_start(out=x_table[1][:], in_=x_rows[1])
+        nc.sync.dma_start(out=w_last[:], in_=w_rows[1])
 
         warm = keep.tile([P, 2], F32, name="warm")
         nc.gpsimd.memset(warm[:, 0:1], 0.0)
@@ -81,11 +82,20 @@ def tile_picked_andpool_none_p_kernel(tc, x_words, x_scales, w1, offs, out):
         w_codes, w_planes = [], []
         for z in range(PASSES):
             w_grouped = keep.tile([P, M, PACK], BF16, name="w_grouped%d" % z, align_bytes=64)
-            parts = ((0, PACK, w_first),) if z == 0 else ((0, EARLY, w_early), (EARLY, PACK, w_last))
-            for t0, t1, raw in parts:
-                nc.scalar.copy(
-                    out=w_grouped[:, :, t0:t1].rearrange("p (c i) t -> p c t i", i=PACK),
-                    in_=raw[:].rearrange("p t (c i) -> p c t i", i=PACK),
+            raw = (w_first, w_last)[z]
+            split = (M, SCALAR_SHARE)[z]
+            nc.scalar.copy(
+                out=w_grouped[:, :split, :].rearrange("p (c i) t -> p c t i", i=PACK),
+                in_=raw[:, :, :split].rearrange("p t (c i) -> p c t i", i=PACK),
+            )
+            if split < M:
+                nc.gpsimd.tensor_scalar(
+                    out=w_grouped[:, split:, :],
+                    in0=raw[:, :, split:].rearrange("p t m -> p m t"),
+                    scalar1=1.0,
+                    scalar2=0.0,
+                    op0=mybir.AluOpType.mult,
+                    op1=mybir.AluOpType.add,
                 )
             tag = "scale_table" if z == 0 else "w_codes"
             w_codes.append(keep.tile([P, M], U32, name="w_codes%d" % z, tag=tag, align_bytes=64))

@@ -24,7 +24,7 @@ STRIPE = 16
 GATHER = 256
 BLOCK = 128
 
-HEAD = T // 8
+HEAD = 3 * T // 8
 SCALAR_SHARE = 72
 SPREAD = 4
 GROUPS = [(first, BLOCK) for first in range(0, S, BLOCK)]
@@ -46,13 +46,13 @@ def tile_picked_andpool_none_p_kernel(tc, x_words, x_scales, w1, offs, out):
         w_first = keep.tile([P, PACK, M], F32, name="w_first")
         w_last = keep.tile([P, PACK, M], F32, name="w_last", align_bytes=64)
         x_rows = [x_words[z].rearrange("p c t -> p (c t)").bitcast(I32) for z in range(PASSES)]
-        nc.sync.dma_start(out=w_first[:], in_=w_rows[0])
-        nc.sync.dma_start(offsets[:], offs)
         nc.sync.dma_start(out=x_table[0][:, :HEAD], in_=x_rows[0][:, :HEAD])
+        nc.sync.dma_start(offsets[:], offs)
         nc.sync.dma_start(
             out=scale_table[::SPREAD, :].bitcast(I32),
             in_=x_scales.rearrange("z b c -> b z c").bitcast(I32),
         )
+        nc.sync.dma_start(out=w_first[:], in_=w_rows[0])
         nc.sync.dma_start(out=x_table[0][:, HEAD:], in_=x_rows[0][:, HEAD:])
         nc.sync.dma_start(out=x_table[1][:], in_=x_rows[1])
         nc.sync.dma_start(out=w_last[:], in_=w_rows[1])
@@ -97,8 +97,7 @@ def tile_picked_andpool_none_p_kernel(tc, x_words, x_scales, w1, offs, out):
                     op0=mybir.AluOpType.mult,
                     op1=mybir.AluOpType.add,
                 )
-            tag = "scale_table" if z == 0 else "w_codes"
-            w_codes.append(keep.tile([P, M], U32, name="w_codes%d" % z, tag=tag, align_bytes=64))
+            w_codes.append(keep.tile([P, M], U32, name="w_codes%d" % z, align_bytes=64))
             w_planes.append(keep.tile([P, M], U8, name="w_plane%d" % z, align_bytes=64))
             nc.vector.quantize_mx(
                 out=w_codes[z][:].bitcast(FP8X4), scales=w_planes[z][:], in_=w_grouped[:].rearrange("p m t -> p (m t)")
@@ -132,7 +131,7 @@ def tile_picked_andpool_none_p_kernel(tc, x_words, x_scales, w1, offs, out):
 
         truth = keep.tile([M, S], F32, name="truth")
         last = S - BLOCK
-        for first in (0, V, BLOCK, 2 * BLOCK, V + BLOCK, last):
+        for first in (0, V, BLOCK, V + BLOCK, 2 * BLOCK, last):
             multiply(sums[first], 1, last_codes[first], first, BLOCK)
             step = BLOCK // 2 if first == last else BLOCK
             for c0 in range(0, BLOCK, step):

@@ -19,15 +19,12 @@ PACK = 4
 PASSES = K // (P * PACK)
 QUADRANT = 32
 ROWS = 4
-PASS_BLOCKS = ROWS * P // QUADRANT
 STRIPE = 16
-GATHER = 256
 BLOCK = 128
-
+SPREAD = 4
+LAST_GATHER = T // 8
 HEAD = 3 * T // 8
 SCALAR_SHARE = 72
-SPREAD = 4
-GROUPS = [(first, BLOCK) for first in range(0, S, BLOCK)]
 
 
 def tile_picked_andpool_none_p_kernel(tc, x_words, x_scales, w1, offs, out):
@@ -39,13 +36,13 @@ def tile_picked_andpool_none_p_kernel(tc, x_words, x_scales, w1, offs, out):
         offsets = keep.tile([P, S // STRIPE], U16, name="offsets")
         x_table = [keep.tile([P, T], I32, name="x_table%d" % z) for z in range(PASSES)]
         scale_table = keep.tile([P, T], U8, name="scale_table", align_bytes=64)
+        w_first = keep.tile([P, PACK, M], F32, name="w_first")
+        w_last = keep.tile([P, PACK, M], F32, name="w_last", align_bytes=64)
 
         nc.vector.memset(scale_table[:].bitcast(I32), 0)
 
-        w_rows = [w1[z * P * PACK : (z + 1) * P * PACK, :].rearrange("(p t) m -> p t m", t=PACK) for z in range(PASSES)]
-        w_first = keep.tile([P, PACK, M], F32, name="w_first")
-        w_last = keep.tile([P, PACK, M], F32, name="w_last", align_bytes=64)
         x_rows = [x_words[z].rearrange("p c t -> p (c t)").bitcast(I32) for z in range(PASSES)]
+        w_rows = [w1[z * P * PACK : (z + 1) * P * PACK, :].rearrange("(p t) m -> p t m", t=PACK) for z in range(PASSES)]
         nc.sync.dma_start(out=x_table[0][:, :HEAD], in_=x_rows[0][:, :HEAD])
         nc.sync.dma_start(offsets[:], offs)
         nc.sync.dma_start(
@@ -65,25 +62,19 @@ def tile_picked_andpool_none_p_kernel(tc, x_words, x_scales, w1, offs, out):
         nc.vector.tensor_copy(out=picked_scales[:], in_=scale_table[:].indirect(offsets[:]))
         x_planes = keep.tile([P, S], U8, name="x_planes", align_bytes=64)
         nc.vector.tensor_copy(out=x_planes[:].bitcast(I32), in_=picked_scales[:].bitcast(I32))
-
-        plane_start = (0, SPREAD)
         for z in range(PASSES):
             for r in range(1, ROWS):
-                at = SPREAD * (PASSES * r + z)
-                to = plane_start[z] + r
                 nc.sync.dma_start(
-                    out=x_planes[to::QUADRANT, :].bitcast(I32),
-                    in_=picked_scales[at::QUADRANT, :].bitcast(I32),
+                    out=x_planes[SPREAD * z + r :: QUADRANT, :].bitcast(I32),
+                    in_=picked_scales[SPREAD * (PASSES * r + z) :: QUADRANT, :].bitcast(I32),
                 )
 
         first_codes = keep.tile([P, S], U32, name="first_codes", align_bytes=64)
         nc.vector.tensor_copy(out=first_codes[:], in_=x_table[0][:].bitcast(U32).indirect(offsets[:]))
 
         w_codes, w_planes = [], []
-        for z in range(PASSES):
+        for z, (raw, split) in enumerate(((w_first, M), (w_last, SCALAR_SHARE))):
             w_grouped = keep.tile([P, M, PACK], BF16, name="w_grouped%d" % z, align_bytes=64)
-            raw = (w_first, w_last)[z]
-            split = (M, SCALAR_SHARE)[z]
             nc.scalar.copy(
                 out=w_grouped[:, :split, :].rearrange("p (c i) t -> p c t i", i=PACK),
                 in_=raw[:, :, :split].rearrange("p t (c i) -> p c t i", i=PACK),
@@ -103,25 +94,25 @@ def tile_picked_andpool_none_p_kernel(tc, x_words, x_scales, w1, offs, out):
                 out=w_codes[z][:].bitcast(FP8X4), scales=w_planes[z][:], in_=w_grouped[:].rearrange("p m t -> p (m t)")
             )
 
-        def multiply(acc, z, codes, first, width):
+        def multiply(acc, z, codes, first):
             nc.tensor.matmul_mx(
                 out=acc[:],
                 lhsT=w_codes[z][:].bitcast(FP8X4),
                 lhsT_scale=w_planes[z][:],
                 rhs=codes.bitcast(FP8X4),
-                rhs_scale=x_planes[plane_start[z] :, first : first + width],
+                rhs_scale=x_planes[SPREAD * z :, first : first + BLOCK],
                 start=(z == 0),
                 stop=(z == PASSES - 1),
             )
 
         sums = {}
-        for first, width in GROUPS:
-            sums[first] = psum.tile([M, width], F32, name="sums%d" % first)
-            multiply(sums[first], 0, first_codes[:, first : first + width], first, width)
+        for first in range(0, S, BLOCK):
+            sums[first] = psum.tile([M, BLOCK], F32, name="sums%d" % first)
+            multiply(sums[first], 0, first_codes[:, first : first + BLOCK], first)
 
         last_codes = {}
-        for g0, g1 in ((0, S - GATHER), (S - GATHER, S)):
-            tag = "w_last" if g1 == S else "last_codes%d" % g0
+        for g0, g1 in ((0, S - LAST_GATHER), (S - LAST_GATHER, S)):
+            tag = "w_last" if g1 == S else "last_codes"
             picked = keep.tile([P, g1 - g0], U32, name="last_codes%d" % g0, tag=tag, align_bytes=64)
             nc.vector.tensor_copy(
                 out=picked[:], in_=x_table[1][:].bitcast(U32).indirect(offsets[:, g0 // STRIPE : g1 // STRIPE])
@@ -130,17 +121,15 @@ def tile_picked_andpool_none_p_kernel(tc, x_words, x_scales, w1, offs, out):
                 last_codes[first] = picked[:, first - g0 : first - g0 + BLOCK]
 
         truth = keep.tile([M, S], F32, name="truth")
-        last = S - BLOCK
-        for first in (0, V, BLOCK, V + BLOCK, 2 * BLOCK, last):
-            multiply(sums[first], 1, last_codes[first], first, BLOCK)
-            step = BLOCK // 2 if first == last else BLOCK
-            for c0 in range(0, BLOCK, step):
-                nc.scalar.activation(
-                    out=truth[:, first + c0 : first + c0 + step], in_=sums[first][:, c0 : c0 + step], func=SIGMOID
-                )
         for v0 in range(0, V, BLOCK):
+            step = BLOCK // 2 if V + v0 >= S - LAST_GATHER else BLOCK
+            for first, width in ((v0, BLOCK), (V + v0, step)):
+                multiply(sums[first], 1, last_codes[first], first)
+                for c0 in range(0, BLOCK, width):
+                    nc.scalar.activation(
+                        out=truth[:, first + c0 : first + c0 + width], in_=sums[first][:, c0 : c0 + width], func=SIGMOID
+                    )
             joined = keep.tile([M, BLOCK], F32, name="joined%d" % v0)
-            step = BLOCK // 2 if V + v0 == last else BLOCK
             for c0 in range(0, BLOCK, step):
                 nc.vector.tensor_mul(
                     out=joined[:, c0 : c0 + step],

@@ -20,9 +20,9 @@ PASSES = K // (P * PACK)
 QUADRANT = 32
 ROWS = 4
 STRIPE = 16
-BLOCK = 128
+STRETCH = 128
 SPREAD = 4
-LAST_GATHER = T // 8
+LAST_GATHER = 2 * STRETCH
 HEAD = 3 * T // 8
 SCALAR_SHARE = 72
 
@@ -55,7 +55,7 @@ def tile_picked_andpool_none_p_kernel(tc, x_words, x_scales, w1, offs, out):
         nc.sync.dma_start(out=w_last[:], in_=w_rows[1])
 
         warm = keep.tile([P, 2], F32, name="warm")
-        nc.gpsimd.memset(warm[:, 0:1], 0.0)
+        nc.vector.memset(warm[:, 0:1], 0.0)
         nc.scalar.activation(out=warm[:, 1:2], in_=warm[:, 0:1], func=SIGMOID)
 
         picked_scales = keep.tile([P, S], U8, name="picked_scales")
@@ -100,15 +100,15 @@ def tile_picked_andpool_none_p_kernel(tc, x_words, x_scales, w1, offs, out):
                 lhsT=w_codes[z][:].bitcast(FP8X4),
                 lhsT_scale=w_planes[z][:],
                 rhs=codes.bitcast(FP8X4),
-                rhs_scale=x_planes[SPREAD * z :, first : first + BLOCK],
+                rhs_scale=x_planes[SPREAD * z :, first : first + STRETCH],
                 start=(z == 0),
                 stop=(z == PASSES - 1),
             )
 
         sums = {}
-        for first in range(0, S, BLOCK):
-            sums[first] = psum.tile([M, BLOCK], F32, name="sums%d" % first)
-            multiply(sums[first], 0, first_codes[:, first : first + BLOCK], first)
+        for first in range(0, S, STRETCH):
+            sums[first] = psum.tile([M, STRETCH], F32, name="sums%d" % first)
+            multiply(sums[first], 0, first_codes[:, first : first + STRETCH], first)
 
         last_codes = {}
         for g0, g1 in ((0, S - LAST_GATHER), (S - LAST_GATHER, S)):
@@ -117,23 +117,23 @@ def tile_picked_andpool_none_p_kernel(tc, x_words, x_scales, w1, offs, out):
             nc.vector.tensor_copy(
                 out=picked[:], in_=x_table[1][:].bitcast(U32).indirect(offsets[:, g0 // STRIPE : g1 // STRIPE])
             )
-            for first in range(g0, g1, BLOCK):
-                last_codes[first] = picked[:, first - g0 : first - g0 + BLOCK]
+            for first in range(g0, g1, STRETCH):
+                last_codes[first] = picked[:, first - g0 : first - g0 + STRETCH]
 
         truth = keep.tile([M, S], F32, name="truth")
-        for v0 in range(0, V, BLOCK):
-            step = BLOCK // 2 if V + v0 >= S - LAST_GATHER else BLOCK
-            for first, width in ((v0, BLOCK), (V + v0, step)):
+        for v0 in range(0, V, STRETCH):
+            step = STRETCH // 2 if V + v0 >= S - LAST_GATHER else STRETCH
+            for first, width in ((v0, STRETCH), (V + v0, step)):
                 multiply(sums[first], 1, last_codes[first], first)
-                for c0 in range(0, BLOCK, width):
+                for c0 in range(0, STRETCH, width):
                     nc.scalar.activation(
                         out=truth[:, first + c0 : first + c0 + width], in_=sums[first][:, c0 : c0 + width], func=SIGMOID
                     )
-            joined = keep.tile([M, BLOCK], F32, name="joined%d" % v0)
-            for c0 in range(0, BLOCK, step):
+            joined = keep.tile([M, STRETCH], F32, name="joined%d" % v0)
+            for c0 in range(0, STRETCH, step):
                 nc.vector.tensor_mul(
                     out=joined[:, c0 : c0 + step],
                     in0=truth[:, v0 + c0 : v0 + c0 + step],
                     in1=truth[:, V + v0 + c0 : V + v0 + c0 + step],
                 )
-            nc.sync.dma_start(out=out[:, v0 : v0 + BLOCK], in_=joined[:])
+            nc.sync.dma_start(out=out[:, v0 : v0 + STRETCH], in_=joined[:])

@@ -24,7 +24,7 @@ STRETCH = 128
 SPREAD = 4
 LAST_GATHER = 2 * STRETCH
 HEAD = 3 * T // 8
-SCALAR_SHARE = 72
+SCALAR_SHARE = 80
 
 
 def tile_picked_andpool_none_p_kernel(tc, x_words, x_scales, w1, offs, out):

@@ -24,7 +24,8 @@ STRETCH = 128
 SPREAD = 4
 LAST_GATHER = 2 * STRETCH
 HEAD = 3 * T // 8
-SCALAR_SHARE = 80
+SCALAR_SHARE = 76
+HALF = M // 2
 
 
 def tile_picked_andpool_none_p_kernel(tc, x_words, x_scales, w1, offs, out):
@@ -72,27 +73,40 @@ def tile_picked_andpool_none_p_kernel(tc, x_words, x_scales, w1, offs, out):
         first_codes = keep.tile([P, S], U32, name="first_codes", align_bytes=64)
         nc.vector.tensor_copy(out=first_codes[:], in_=x_table[0][:].bitcast(U32).indirect(offsets[:]))
 
-        w_codes, w_planes = [], []
-        for z, (raw, split) in enumerate(((w_first, M), (w_last, SCALAR_SHARE))):
-            w_grouped = keep.tile([P, M, PACK], BF16, name="w_grouped%d" % z, align_bytes=64)
+        def round_on_scalar(grouped, raw):
             nc.scalar.copy(
-                out=w_grouped[:, :split, :].rearrange("p (c i) t -> p c t i", i=PACK),
-                in_=raw[:, :, :split].rearrange("p t (c i) -> p c t i", i=PACK),
+                out=grouped.rearrange("p (c i) t -> p c t i", i=PACK),
+                in_=raw.rearrange("p t (c i) -> p c t i", i=PACK),
             )
-            if split < M:
-                nc.gpsimd.tensor_scalar(
-                    out=w_grouped[:, split:, :],
-                    in0=raw[:, :, split:].rearrange("p t m -> p m t"),
-                    scalar1=1.0,
-                    scalar2=0.0,
-                    op0=mybir.AluOpType.mult,
-                    op1=mybir.AluOpType.add,
-                )
-            w_codes.append(keep.tile([P, M], U32, name="w_codes%d" % z, align_bytes=64))
-            w_planes.append(keep.tile([P, M], U8, name="w_plane%d" % z, align_bytes=64))
+
+        def quantise(z, m0, grouped):
+            m1 = m0 + grouped.shape[1]
             nc.vector.quantize_mx(
-                out=w_codes[z][:].bitcast(FP8X4), scales=w_planes[z][:], in_=w_grouped[:].rearrange("p m t -> p (m t)")
+                out=w_codes[z][:, m0:m1].bitcast(FP8X4),
+                scales=w_planes[z][:, m0:m1],
+                in_=grouped[:].rearrange("p m t -> p (m t)"),
             )
+
+        w_codes = [keep.tile([P, M], U32, name="w_codes%d" % z, align_bytes=64) for z in range(PASSES)]
+        w_planes = [keep.tile([P, M], U8, name="w_plane%d" % z, align_bytes=64) for z in range(PASSES)]
+        first_grouped = keep.tile([P, M, PACK], BF16, name="first_grouped", align_bytes=64)
+        round_on_scalar(first_grouped[:], w_first[:])
+        quantise(0, 0, first_grouped)
+
+        lower = keep.tile([P, HALF, PACK], BF16, name="lower", align_bytes=64)
+        upper = keep.tile([P, HALF, PACK], BF16, name="upper", align_bytes=64)
+        round_on_scalar(lower[:], w_last[:, :, :HALF])
+        round_on_scalar(upper[:, : SCALAR_SHARE - HALF, :], w_last[:, :, HALF:SCALAR_SHARE])
+        nc.gpsimd.tensor_scalar(
+            out=upper[:, SCALAR_SHARE - HALF :, :],
+            in0=w_last[:, :, SCALAR_SHARE:].rearrange("p t m -> p m t"),
+            scalar1=1.0,
+            scalar2=0.0,
+            op0=mybir.AluOpType.mult,
+            op1=mybir.AluOpType.add,
+        )
+        quantise(1, 0, lower)
+        quantise(1, HALF, upper)
 
         def multiply(acc, z, codes, first):
             nc.tensor.matmul_mx(

@@ -128,9 +128,12 @@ def tile_picked_andpool_none_p_kernel(tc, x_words, x_scales, w1, offs, out):
         for g0, g1 in ((0, S - LAST_GATHER), (S - LAST_GATHER, S)):
             tag = "w_last" if g1 == S else "last_codes"
             picked = keep.tile([P, g1 - g0], U32, name="last_codes%d" % g0, tag=tag, align_bytes=64)
-            nc.vector.tensor_copy(
-                out=picked[:], in_=x_table[1][:].bitcast(U32).indirect(offsets[:, g0 // STRIPE : g1 // STRIPE])
-            )
+            step = STRETCH if g1 == S else g1 - g0
+            for e0 in range(g0, g1, step):
+                nc.vector.tensor_copy(
+                    out=picked[:, e0 - g0 : e0 - g0 + step],
+                    in_=x_table[1][:].bitcast(U32).indirect(offsets[:, e0 // STRIPE : (e0 + step) // STRIPE]),
+                )
             for first in range(g0, g1, STRETCH):
                 last_codes[first] = picked[:, first - g0 : first - g0 + STRETCH]
 

@@ -61,12 +61,15 @@ def tile_picked_andpool_none_p_kernel(tc, x_words, x_scales, w1, offs, out):
 
         picked_scales = keep.tile([P, S], U8, name="picked_scales")
         nc.vector.tensor_copy(out=picked_scales[:], in_=scale_table[:].indirect(offsets[:]))
-        x_planes = keep.tile([P, S], U8, name="x_planes", align_bytes=64)
-        nc.vector.tensor_copy(out=x_planes[:].bitcast(I32), in_=picked_scales[:].bitcast(I32))
+        x_planes = keep.tile([P, PASSES, S], U8, name="x_planes", align_bytes=64)
+        nc.vector.tensor_copy(
+            out=x_planes[:].bitcast(I32),
+            in_=picked_scales[:].bitcast(I32).unsqueeze(1).to_broadcast([P, PASSES, S // 4]),
+        )
         for z in range(PASSES):
             for r in range(1, ROWS):
                 nc.sync.dma_start(
-                    out=x_planes[SPREAD * z + r :: QUADRANT, :].bitcast(I32),
+                    out=x_planes[SPREAD * z + r :: QUADRANT, z, :].bitcast(I32),
                     in_=picked_scales[SPREAD * (PASSES * r + z) :: QUADRANT, :].bitcast(I32),
                 )
 
@@ -114,7 +117,7 @@ def tile_picked_andpool_none_p_kernel(tc, x_words, x_scales, w1, offs, out):
                 lhsT=w_codes[z][:].bitcast(FP8X4),
                 lhsT_scale=w_planes[z][:],
                 rhs=codes.bitcast(FP8X4),
-                rhs_scale=x_planes[SPREAD * z :, first : first + STRETCH],
+                rhs_scale=x_planes[SPREAD * z :, z, first : first + STRETCH],
                 start=(z == 0),
                 stop=(z == PASSES - 1),
             )
@@ -139,7 +142,7 @@ def tile_picked_andpool_none_p_kernel(tc, x_words, x_scales, w1, offs, out):
 
         truth = keep.tile([M, S], F32, name="truth")
         for v0 in range(0, V, STRETCH):
-            step = STRETCH // 2 if V + v0 >= S - LAST_GATHER else STRETCH
+            step = STRETCH // 2 if v0 + STRETCH == V else STRETCH
             for first, width in ((v0, STRETCH), (V + v0, step)):
                 multiply(sums[first], 1, last_codes[first], first)
                 for c0 in range(0, STRETCH, width):

@@ -22,6 +22,7 @@ ROWS = 4
 STRIPE = 16
 STRETCH = 128
 SPREAD = 4
+LINE = 256
 LAST_GATHER = 2 * STRETCH
 HEAD = 3 * T // 8
 SCALAR_SHARE = 76
@@ -34,11 +35,11 @@ def tile_picked_andpool_none_p_kernel(tc, x_words, x_scales, w1, offs, out):
         keep = ctx.enter_context(tc.tile_pool(name="keep", bufs=1))
         psum = ctx.enter_context(tc.psum_pool(name="psum", bufs=1))
 
-        offsets = keep.tile([P, S // STRIPE], U16, name="offsets")
-        x_table = [keep.tile([P, T], I32, name="x_table%d" % z) for z in range(PASSES)]
-        scale_table = keep.tile([P, T], U8, name="scale_table", align_bytes=64)
-        w_first = keep.tile([P, PACK, M], F32, name="w_first")
-        w_last = keep.tile([P, PACK, M], F32, name="w_last", align_bytes=64)
+        offsets = keep.tile([P, S // STRIPE], U16, name="offsets", align_bytes=LINE)
+        x_table = [keep.tile([P, T], I32, name="x_table%d" % z, align_bytes=LINE) for z in range(PASSES)]
+        scale_table = keep.tile([P, T], U8, name="scale_table", align_bytes=LINE)
+        w_first = keep.tile([P, PACK, M], F32, name="w_first", align_bytes=LINE)
+        w_last = keep.tile([P, PACK, M], F32, name="w_last", align_bytes=LINE)
 
         nc.vector.memset(scale_table[:].bitcast(I32), 0)
 
@@ -59,9 +60,9 @@ def tile_picked_andpool_none_p_kernel(tc, x_words, x_scales, w1, offs, out):
         nc.vector.memset(warm[:, 0:1], 0.0)
         nc.scalar.activation(out=warm[:, 1:2], in_=warm[:, 0:1], func=SIGMOID)
 
-        picked_scales = keep.tile([P, S], U8, name="picked_scales")
+        picked_scales = keep.tile([P, S], U8, name="picked_scales", align_bytes=LINE)
         nc.vector.tensor_copy(out=picked_scales[:], in_=scale_table[:].indirect(offsets[:]))
-        x_planes = keep.tile([P, PASSES, S], U8, name="x_planes", align_bytes=64)
+        x_planes = keep.tile([P, PASSES, S], U8, name="x_planes", align_bytes=LINE)
         nc.vector.tensor_copy(
             out=x_planes[:].bitcast(I32),
             in_=picked_scales[:].bitcast(I32).unsqueeze(1).to_broadcast([P, PASSES, S // 4]),
@@ -130,7 +131,7 @@ def tile_picked_andpool_none_p_kernel(tc, x_words, x_scales, w1, offs, out):
         last_codes = {}
         for g0, g1 in ((0, S - LAST_GATHER), (S - LAST_GATHER, S)):
             tag = "w_last" if g1 == S else "last_codes"
-            picked = keep.tile([P, g1 - g0], U32, name="last_codes%d" % g0, tag=tag, align_bytes=64)
+            picked = keep.tile([P, g1 - g0], U32, name="last_codes%d" % g0, tag=tag, align_bytes=LINE)
             step = STRETCH if g1 == S else g1 - g0
             for e0 in range(g0, g1, step):
                 nc.vector.tensor_copy(
@@ -149,7 +150,7 @@ def tile_picked_andpool_none_p_kernel(tc, x_words, x_scales, w1, offs, out):
                     nc.scalar.activation(
                         out=truth[:, first + c0 : first + c0 + width], in_=sums[first][:, c0 : c0 + width], func=SIGMOID
                     )
-            joined = keep.tile([M, STRETCH], F32, name="joined%d" % v0)
+            joined = keep.tile([M, STRETCH], F32, name="joined%d" % v0, align_bytes=LINE)
             for c0 in range(0, STRETCH, step):
                 nc.vector.tensor_mul(
                     out=joined[:, c0 : c0 + step],

@@ -21,10 +21,10 @@ QUADRANT = 32
 ROWS = 4
 STRIPE = 16
 STRETCH = 128
-SPREAD = 4
+SPREAD = 2
+FIRST_ROW = 32
 LINE = 256
 LAST_GATHER = 2 * STRETCH
-HEAD = 3 * T // 8
 SCALAR_SHARE = 76
 HALF = M // 2
 
@@ -45,14 +45,16 @@ def tile_picked_andpool_none_p_kernel(tc, x_words, x_scales, w1, offs, out):
 
         x_rows = [x_words[z].rearrange("p c t -> p (c t)").bitcast(I32) for z in range(PASSES)]
         w_rows = [w1[z * P * PACK : (z + 1) * P * PACK, :].rearrange("(p t) m -> p t m", t=PACK) for z in range(PASSES)]
-        nc.sync.dma_start(out=x_table[0][:, :HEAD], in_=x_rows[0][:, :HEAD])
+        nc.sync.dma_start(out=x_table[0][0::4, :], in_=x_rows[0][0::4, :])
+        nc.sync.dma_start(out=w_first[0::2], in_=w_rows[0][0::2])
         nc.sync.dma_start(offsets[:], offs)
         nc.sync.dma_start(
-            out=scale_table[::SPREAD, :].bitcast(I32),
+            out=scale_table[FIRST_ROW : FIRST_ROW + SPREAD * QUADRANT : SPREAD, :].bitcast(I32),
             in_=x_scales.rearrange("z b c -> b z c").bitcast(I32),
         )
-        nc.sync.dma_start(out=w_first[:], in_=w_rows[0])
-        nc.sync.dma_start(out=x_table[0][:, HEAD:], in_=x_rows[0][:, HEAD:])
+        nc.sync.dma_start(out=w_first[1::2], in_=w_rows[0][1::2])
+        nc.sync.dma_start(out=x_table[0][2::4, :], in_=x_rows[0][2::4, :])
+        nc.sync.dma_start(out=x_table[0][1::2, :], in_=x_rows[0][1::2, :])
         nc.sync.dma_start(out=x_table[1][:], in_=x_rows[1])
         nc.sync.dma_start(out=w_last[:], in_=w_rows[1])
 
@@ -62,17 +64,13 @@ def tile_picked_andpool_none_p_kernel(tc, x_words, x_scales, w1, offs, out):
 
         picked_scales = keep.tile([P, S], U8, name="picked_scales", align_bytes=LINE)
         nc.vector.tensor_copy(out=picked_scales[:], in_=scale_table[:].indirect(offsets[:]))
-        x_planes = keep.tile([P, PASSES, S], U8, name="x_planes", align_bytes=LINE)
-        nc.vector.tensor_copy(
-            out=x_planes[:].bitcast(I32),
-            in_=picked_scales[:].bitcast(I32).unsqueeze(1).to_broadcast([P, PASSES, S // 4]),
-        )
-        for z in range(PASSES):
-            for r in range(1, ROWS):
-                nc.sync.dma_start(
-                    out=x_planes[SPREAD * z + r :: QUADRANT, z, :].bitcast(I32),
-                    in_=picked_scales[SPREAD * (PASSES * r + z) :: QUADRANT, :].bitcast(I32),
-                )
+        x_planes = keep.tile([P, S], U8, name="x_planes", align_bytes=LINE)
+        for r in range(ROWS):
+            row = FIRST_ROW + SPREAD * PASSES * r
+            nc.sync.dma_start(
+                out=x_planes[r::ROWS, :].bitcast(I32),
+                in_=picked_scales[row : row + SPREAD * QUADRANT : SPREAD, :].bitcast(I32),
+            )
 
         first_codes = keep.tile([P, S], U32, name="first_codes", align_bytes=64)
         nc.vector.tensor_copy(out=first_codes[:], in_=x_table[0][:].bitcast(U32).indirect(offsets[:]))
@@ -118,7 +116,7 @@ def tile_picked_andpool_none_p_kernel(tc, x_words, x_scales, w1, offs, out):
                 lhsT=w_codes[z][:].bitcast(FP8X4),
                 lhsT_scale=w_planes[z][:],
                 rhs=codes.bitcast(FP8X4),
-                rhs_scale=x_planes[SPREAD * z :, z, first : first + STRETCH],
+                rhs_scale=x_planes[ROWS * z :, first : first + STRETCH],
                 start=(z == 0),
                 stop=(z == PASSES - 1),
             )

from contextlib import ExitStack

import concourse.mybir as mybir

K, T, S, V, M = 1024, 2048, 768, 384, 128
FLOPS = 2 * K * M * S

F32 = mybir.dt.float32
BF16 = mybir.dt.bfloat16
I32 = mybir.dt.int32
U32 = mybir.dt.uint32
U16 = mybir.dt.uint16
U8 = mybir.dt.uint8
FP8X4 = mybir.dt.float8_e4m3fn_x4
SIGMOID = mybir.ActivationFunctionType.Sigmoid

P = 128
PACK = 4
PASSES = K // (P * PACK)
QUADRANT = 32
ROWS = 4
STRIPE = 16
STRETCH = 128
SPREAD = 2
FIRST_ROW = 32
LINE = 256
LAST_GATHER = 2 * STRETCH
SCALAR_SHARE = 76
HALF = M // 2


def tile_picked_andpool_none_p_kernel(tc, x_words, x_scales, w1, offs, out):
    nc = tc.nc
    with ExitStack() as ctx:
        keep = ctx.enter_context(tc.tile_pool(name="keep", bufs=1))
        psum = ctx.enter_context(tc.psum_pool(name="psum", bufs=1))

        offsets = keep.tile([P, S // STRIPE], U16, name="offsets", align_bytes=LINE)
        x_table = [keep.tile([P, T], I32, name="x_table%d" % z, align_bytes=LINE) for z in range(PASSES)]
        scale_table = keep.tile([P, T], U8, name="scale_table", align_bytes=LINE)
        w_first = keep.tile([P, PACK, M], F32, name="w_first", align_bytes=LINE)
        w_last = keep.tile([P, PACK, M], F32, name="w_last", align_bytes=LINE)

        nc.vector.memset(scale_table[:].bitcast(I32), 0)

        x_rows = [x_words[z].rearrange("p c t -> p (c t)").bitcast(I32) for z in range(PASSES)]
        w_rows = [w1[z * P * PACK : (z + 1) * P * PACK, :].rearrange("(p t) m -> p t m", t=PACK) for z in range(PASSES)]
        nc.sync.dma_start(out=x_table[0][0::4, :], in_=x_rows[0][0::4, :])
        nc.sync.dma_start(out=w_first[0::2], in_=w_rows[0][0::2])
        nc.sync.dma_start(offsets[:], offs)
        nc.sync.dma_start(
            out=scale_table[FIRST_ROW : FIRST_ROW + SPREAD * QUADRANT : SPREAD, :].bitcast(I32),
            in_=x_scales.rearrange("z b c -> b z c").bitcast(I32),
        )
        nc.sync.dma_start(out=w_first[1::2], in_=w_rows[0][1::2])
        nc.sync.dma_start(out=x_table[0][2::4, :], in_=x_rows[0][2::4, :])
        nc.sync.dma_start(out=x_table[0][1::2, :], in_=x_rows[0][1::2, :])
        nc.sync.dma_start(out=x_table[1][:], in_=x_rows[1])
        nc.sync.dma_start(out=w_last[:], in_=w_rows[1])

        warm = keep.tile([P, 2], F32, name="warm")
        nc.vector.memset(warm[:, 0:1], 0.0)
        nc.scalar.activation(out=warm[:, 1:2], in_=warm[:, 0:1], func=SIGMOID)

        picked_scales = keep.tile([P, S], U8, name="picked_scales", align_bytes=LINE)
        nc.vector.tensor_copy(out=picked_scales[:], in_=scale_table[:].indirect(offsets[:]))
        x_planes = keep.tile([P, S], U8, name="x_planes", align_bytes=LINE)
        for r in range(ROWS):
            row = FIRST_ROW + SPREAD * PASSES * r
            nc.sync.dma_start(
                out=x_planes[r::ROWS, :].bitcast(I32),
                in_=picked_scales[row : row + SPREAD * QUADRANT : SPREAD, :].bitcast(I32),
            )

        first_codes = keep.tile([P, S], U32, name="first_codes", align_bytes=64)
        nc.vector.tensor_copy(out=first_codes[:], in_=x_table[0][:].bitcast(U32).indirect(offsets[:]))

        def round_on_scalar(grouped, raw):
            nc.scalar.copy(
                out=grouped.rearrange("p (c i) t -> p c t i", i=PACK),
                in_=raw.rearrange("p t (c i) -> p c t i", i=PACK),
            )

        def quantise(z, m0, grouped):
            m1 = m0 + grouped.shape[1]
            nc.vector.quantize_mx(
                out=w_codes[z][:, m0:m1].bitcast(FP8X4),
                scales=w_planes[z][:, m0:m1],
                in_=grouped[:].rearrange("p m t -> p (m t)"),
            )

        w_codes = [keep.tile([P, M], U32, name="w_codes%d" % z, align_bytes=64) for z in range(PASSES)]
        w_planes = [keep.tile([P, M], U8, name="w_plane%d" % z, align_bytes=64) for z in range(PASSES)]
        first_grouped = keep.tile([P, M, PACK], BF16, name="first_grouped", align_bytes=64)
        round_on_scalar(first_grouped[:], w_first[:])
        quantise(0, 0, first_grouped)

        lower = keep.tile([P, HALF, PACK], BF16, name="lower", align_bytes=64)
        upper = keep.tile([P, HALF, PACK], BF16, name="upper", align_bytes=64)
        round_on_scalar(lower[:], w_last[:, :, :HALF])
        round_on_scalar(upper[:, : SCALAR_SHARE - HALF, :], w_last[:, :, HALF:SCALAR_SHARE])
        nc.gpsimd.tensor_scalar(
            out=upper[:, SCALAR_SHARE - HALF :, :],
            in0=w_last[:, :, SCALAR_SHARE:].rearrange("p t m -> p m t"),
            scalar1=1.0,
            scalar2=0.0,
            op0=mybir.AluOpType.mult,
            op1=mybir.AluOpType.add,
        )
        quantise(1, 0, lower)
        quantise(1, HALF, upper)

        def multiply(acc, z, codes, first):
            nc.tensor.matmul_mx(
                out=acc[:],
                lhsT=w_codes[z][:].bitcast(FP8X4),
                lhsT_scale=w_planes[z][:],
                rhs=codes.bitcast(FP8X4),
                rhs_scale=x_planes[ROWS * z :, first : first + STRETCH],
                start=(z == 0),
                stop=(z == PASSES - 1),
            )

        sums = {}
        for first in range(0, S, STRETCH):
            sums[first] = psum.tile([M, STRETCH], F32, name="sums%d" % first)
            multiply(sums[first], 0, first_codes[:, first : first + STRETCH], first)

        last_codes = {}
        for g0, g1 in ((0, S - LAST_GATHER), (S - LAST_GATHER, S)):
            tag = "w_last" if g1 == S else "last_codes"
            picked = keep.tile([P, g1 - g0], U32, name="last_codes%d" % g0, tag=tag, align_bytes=LINE)
            step = STRETCH if g1 == S else g1 - g0
            for e0 in range(g0, g1, step):
                nc.vector.tensor_copy(
                    out=picked[:, e0 - g0 : e0 - g0 + step],
                    in_=x_table[1][:].bitcast(U32).indirect(offsets[:, e0 // STRIPE : (e0 + step) // STRIPE]),
                )
            for first in range(g0, g1, STRETCH):
                last_codes[first] = picked[:, first - g0 : first - g0 + STRETCH]

        truth = keep.tile([M, S], F32, name="truth")
        for v0 in range(0, V, STRETCH):
            step = STRETCH // 2 if v0 + STRETCH == V else STRETCH
            for first, width in ((v0, STRETCH), (V + v0, step)):
                multiply(sums[first], 1, last_codes[first], first)
                for c0 in range(0, STRETCH, width):
                    nc.scalar.activation(
                        out=truth[:, first + c0 : first + c0 + width], in_=sums[first][:, c0 : c0 + width], func=SIGMOID
                    )
            joined = keep.tile([M, STRETCH], F32, name="joined%d" % v0, align_bytes=LINE)
            for c0 in range(0, STRETCH, step):
                nc.vector.tensor_mul(
                    out=joined[:, c0 : c0 + step],
                    in0=truth[:, v0 + c0 : v0 + c0 + step],
                    in1=truth[:, V + v0 + c0 : V + v0 + c0 + step],
                )
            nc.sync.dma_start(out=out[:, v0 : v0 + STRETCH], in_=joined[:])
